import numpy as np
import ml_dtypes


def mxq(x, axis, fmt="e4m3"):
    dtype, down = {"e4m3": (ml_dtypes.float8_e4m3fn, 7), "e5m2": (ml_dtypes.float8_e5m2, 14)}[fmt]
    v = np.moveaxis(np.asarray(x, np.float32).astype(ml_dtypes.bfloat16).astype(np.float64), axis, -1)
    blocks = v.reshape(v.shape[:-1] + (-1, 32))
    amax = np.abs(blocks).max(-1, keepdims=True)
    byte = np.maximum(np.where(amax > 0, np.frexp(amax)[1] - 1 + 127, 0) - down, 1)
    scale = np.exp2(byte - 127.0)
    codes = (blocks / scale).astype(np.float32).astype(dtype).astype(np.float64)
    return np.moveaxis((codes * scale).reshape(v.shape), -1, axis)


WIDE = False


def mx_kscale(k):
    if not WIDE:
        return np.ones(k)
    levels = np.array([10, -10, 5, -5, 0])
    if k % 512:
        return np.exp2(np.random.permutation(np.resize(levels, k // 32))).repeat(32)
    a = np.empty((k // 512, 16))
    for p in range(k // 512):
        a[p, :8] = np.random.permutation(np.resize(levels, 8))
        for g in range(8):
            far = levels[np.abs(levels - a[p, g]) >= 10]
            a[p, g + 8] = far[np.random.randint(len(far))]
    return np.exp2(a.ravel()).repeat(32)


def f64(x):
    return np.asarray(x).astype(np.float64)


def striped(idx):
    return np.tile(idx.reshape(-1, 16).T, (8, 1)).astype(np.uint16)


def unstriped(offs):
    return offs[:16].T.reshape(-1).astype(np.int64)


E2M1 = np.array([0.0, 0.5, 1.0, 1.5, 2.0, 3.0, 4.0, 6.0, -0.0, -0.5, -1.0, -1.5, -2.0, -3.0, -4.0, -6.0])


def pack_weight(w, fmt):
    k, n = w.shape
    w = f64(np.asarray(w, np.float32).astype(ml_dtypes.bfloat16)).reshape(k // 32, 32, n)
    amax = np.abs(w).max(1)
    if fmt == "e4m3":
        byte = np.frexp(amax)[1] - 1 + 127 - 7
    else:
        mant, ex = np.frexp(amax / 6.0)
        byte = np.where(mant > 0.5, ex, ex - 1) + 127
    byte = np.clip(np.where(amax > 0, byte, 1), 1, 254)
    scaled = (w * np.exp2(127.0 - byte)[:, None, :]).reshape(k, n).astype(np.float32)
    by_word = np.ascontiguousarray(scaled.reshape(k // 512, 128, 4, n).transpose(0, 1, 3, 2))
    if fmt == "e4m3":
        words = by_word.astype(ml_dtypes.float8_e4m3fn).view(np.uint8)
    else:
        c = by_word.astype(ml_dtypes.float4_e2m1fn).view(np.uint8) & 0xF
        words = (c[..., 0::2] | (c[..., 1::2] << 4)).reshape(k // 512, 128, 2 * n)
    return np.ascontiguousarray(words), np.ascontiguousarray(byte.astype(np.uint8).reshape(k // 512, 16, n))


def unpack_weight(words, scales, fmt):
    g, _, n = scales.shape
    words = np.ascontiguousarray(words).reshape(g, 128, n, -1)
    if fmt == "e4m3":
        vals = words.view(ml_dtypes.float8_e4m3fn).astype(np.float64)
    else:
        nib = np.empty((g, 128, n, 4), np.uint8)
        nib[..., 0::2] = words & 0xF
        nib[..., 1::2] = words >> 4
        vals = E2M1[nib]
    vals = vals * np.repeat(np.exp2(scales.astype(np.float64) - 127.0), 8, axis=1)[..., None]
    return vals.transpose(0, 1, 3, 2).reshape(g * 512, n)


def gelu(v):
    return 0.5 * v * (1.0 + np.tanh(np.sqrt(2.0 / np.pi) * (v + 0.044715 * v**3)))


K, H, N, T, S, T2, P = 1024, 1024, 512, 4096, 1024, 2048, 1024

def setup_inputs():
    n = np.random.standard_normal
    s = mx_kscale(K)[:, None]
    u = mx_kscale(H)[:, None]
    tab_words, tab_scales = pack_weight(n((K, T)) * s, "e4m3")
    w1_words, w1_scales = pack_weight(0.7 * n((K, H)) / np.sqrt(K) / s, "e2m1")
    return {
        "tab_words": tab_words, "tab_scales": tab_scales,
        "offs": striped(np.random.permutation(T)[:S]),
        "offs2": striped(np.random.permutation(T2)[:S]),
        "offs3": striped(np.random.permutation(T2)[:P]),
        "w1_words": w1_words, "w1_scales": w1_scales,
        "stock": (0.5 * n((H, S))).astype(np.float32),
        "page0": (0.8 * n((H, T2))).astype(np.float32),
        "wgs": np.exp(0.3 * n((128, S))).astype(np.float32),
        "temp": np.random.uniform(0.4, 1.6, H).astype(np.float32),
        "plan": (0.12 * n((H, P))).astype(np.float32),
        "gain": (np.random.choice([-1.0, 1.0], H) * np.random.uniform(2.5, 5.0, H) * u[:, 0]).astype(np.float32),
        "w4": (n((H, N)) / np.sqrt(H) / u).astype(np.float32),
        "floor": (0.5 * n(N)).astype(np.float32),
    }

def reference(tab_words, tab_scales, offs, offs2, offs3, w1_words, w1_scales, stock, page0, wgs, temp, plan, gain, w4, floor):
    v = unpack_weight(tab_words, tab_scales, "e4m3")[:, unstriped(offs)]
    w1 = unpack_weight(w1_words, w1_scales, "e2m1")
    h = (w1.T @ v) + f64(stock)
    page = f64(page0).copy()
    page[:, unstriped(offs2)] = np.tile(f64(wgs), (H // 128, 1)) * h
    top = page.max(axis=1)
    a = np.exp(f64(temp)[:, None] * (page[:, unstriped(offs3)] - top[:, None]))
    f = f64(gain)[:, None] * (a - f64(plan))
    y = mxq(f64(w4), 0, "e4m3").T @ mxq(f, 0, "e4m3")
    return np.maximum(y, f64(floor)[:, None])

@@ -1,0 +1,277 @@
+from contextlib import ExitStack
+
+import concourse.mybir as mybir
+
+K, H, N, T, S, T2, PW = 1024, 1024, 512, 4096, 1024, 2048, 1024
+FLOPS = 2 * K * H * S + 2 * H * N * PW
+
+F32 = mybir.dt.float32
+BF16 = mybir.dt.bfloat16
+I32 = mybir.dt.int32
+U32 = mybir.dt.uint32
+U16 = mybir.dt.uint16
+U8 = mybir.dt.uint8
+FP8X4 = mybir.dt.float8_e4m3fn_x4
+FP4X4 = mybir.dt.float4_e2m1fn_x4
+ALU = mybir.AluOpType
+ACT = mybir.ActivationFunctionType
+AX = mybir.AxisListType
+
+P = 128
+PACK = 4
+PASSES = 2
+TILES = PASSES * PACK
+HALF = 512
+LIST_HALF = HALF // 16
+F32_MAX = 3.4028234663852886e38
+
+
+def tile_list_wave_bin_scores_kernel(
+    tc, tab_words, tab_scales, offs, offs2, offs3, w1_words, w1_scales,
+    stock, page0, wgs, temp, plan, gain, w4, floor, out,
+):
+    nc = tc.nc
+    with ExitStack() as ctx:
+        lists = ctx.enter_context(tc.tile_pool(name="lists", bufs=1))
+        keep = ctx.enter_context(tc.tile_pool(name="keep", bufs=1))
+        ring2 = ctx.enter_context(tc.tile_pool(name="ring2", bufs=2))
+        ring3 = ctx.enter_context(tc.tile_pool(name="ring3", bufs=3))
+        ring4 = ctx.enter_context(tc.tile_pool(name="ring4", bufs=4))
+        psum = ctx.enter_context(tc.psum_pool(name="psum", bufs=1))
+
+        def rows(mat, t):
+            return mat.rearrange("(b p i) c -> b i p c", b=PASSES, i=PACK)[t // PACK, t % PACK]
+
+        def half(h):
+            return slice(h * HALF, (h + 1) * HALF)
+
+        def list_half(h):
+            return slice(h * LIST_HALF, (h + 1) * LIST_HALF)
+
+        idx1 = lists.tile([P, S // 16], U16, name="idx1")
+        idx2 = lists.tile([P, S // 16], U16, name="idx2")
+        idx3 = lists.tile([P, PW // 16], U16, name="idx3")
+        nc.sync.dma_start(idx1[:], offs)
+        nc.sync.dma_start(idx2[:], offs2)
+
+        w1s_raw = keep.tile([P, PASSES, H], U8, name="w1s_raw", align_bytes=64)
+        nc.vector.memset(w1s_raw[:].bitcast(I32), 0)
+        tabs = keep.tile([P, T], U8, name="tabs", align_bytes=64)
+        nc.vector.memset(tabs[0:96, :].bitcast(I32), 0)
+        nc.sync.dma_start(tabs[96:128, :].bitcast(I32), tab_scales.rearrange("a q t -> (a q) t").bitcast(I32))
+        for q in range(4):
+            nc.scalar.dma_start(
+                w1s_raw[32 * q : 32 * q + 4, :, :].bitcast(I32),
+                w1_scales[:, 4 * q : 4 * q + 4, :].rearrange("a r c -> r a c").bitcast(I32),
+            )
+        w1w_raw = keep.tile([P, PASSES, 2 * H], U8, name="w1w_raw", align_bytes=64)
+        nc.sync.dma_start(w1w_raw[:].bitcast(I32), w1_words.rearrange("a p n -> p a n").bitcast(I32))
+        tabw = []
+        for a in range(PASSES):
+            tw = keep.tile([P, T], U32, name="tabw%d" % a, tag="tabw%d" % a, align_bytes=64)
+            nc.sync.dma_start(tw[:].bitcast(I32), tab_words[a].rearrange("p t i -> p (t i)").bitcast(I32))
+            tabw.append(tw)
+
+        vs = keep.tile([P, PASSES, S], U8, name="vs", align_bytes=64)
+        nc.gpsimd.memset(vs[:], 0)
+        gs = keep.tile([P, S], U8, name="gs", align_bytes=64)
+        nc.vector.tensor_copy(gs[:], tabs[:].indirect(idx1[:]))
+        for a in range(PASSES):
+            for q in range(4):
+                src = 96 + 16 * a + 4 * q
+                nc.scalar.dma_start(vs[32 * q : 32 * q + 4, a, :].bitcast(I32), gs[src : src + 4, :].bitcast(I32))
+
+        w1w = keep.tile([P, PASSES, 2 * H], U8, name="w1w", align_bytes=64)
+        for a in range(PASSES):
+            nc.vector.tensor_copy(
+                w1w[:, a, :].rearrange("p (b i m e) -> p b i m e", b=PASSES, i=PACK, e=2),
+                w1w_raw[:, a, :].rearrange("p (b m i e) -> p b i m e", b=PASSES, i=PACK, e=2),
+            )
+        w1s = keep.tile([P, PASSES, H], U8, name="w1s", align_bytes=64)
+        nc.vector.tensor_copy(
+            w1s[:].rearrange("p a (b i m) -> p (a b) i m", b=PASSES, i=PACK),
+            w1s_raw[:].rearrange("p a (b m i) -> p (a b) i m", b=PASSES, i=PACK),
+        )
+
+        vw = [[None, None], [None, None]]
+        for a in range(PASSES):
+            for h in range(2):
+                g = keep.tile([P, HALF], U32, name="vw%d%d" % (a, h), align_bytes=64)
+                nc.vector.tensor_copy(g[:], tabw[a][:].indirect(idx1[:, list_half(h)]))
+                vw[a][h] = g
+
+        stock_t, wgs_t, page_t, plan_t = {}, {}, {}, {}
+
+        def load_front(t):
+            stock_t[t] = ring3.tile([P, S], F32, name="stock")
+            nc.sync.dma_start(stock_t[t][:], rows(stock, t))
+            if t < PACK:
+                wgs_t[t] = keep.tile([P, S], F32, name="wgs%d" % t, tag="wgs%d" % t, align_bytes=64)
+                for q in range(4):
+                    nc.sync.dma_start(
+                        wgs_t[t][32 * q : 32 * q + 32, :], wgs.rearrange("(u i) c -> i u c", i=PACK)[t]
+                    )
+            page_t[t] = ring4.tile([P, T2], F32, name="page")
+            nc.sync.dma_start(page_t[t][:], rows(page0, t))
+
+        def load_plan(t):
+            plan_t[t] = ring3.tile([P, PW], F32, name="plan")
+            nc.sync.dma_start(plan_t[t][:], rows(plan, t))
+
+        stock0, wgs0 = [], []
+        for h in range(2):
+            st = keep.tile([P, HALF], F32, name="stock0_%d" % h)
+            nc.sync.dma_start(st[:], rows(stock, 0)[:, half(h)])
+            wg = keep.tile([P, HALF], F32, name="wgs0_%d" % h)
+            for q in range(4):
+                nc.sync.dma_start(
+                    wg[32 * q : 32 * q + 32, :], wgs.rearrange("(u i) c -> i u c", i=PACK)[0][:, half(h)]
+                )
+            if h == 0:
+                page_t[0] = ring4.tile([P, T2], F32, name="page")
+                nc.sync.dma_start(page_t[0][:], rows(page0, 0))
+            stock0.append(st)
+            wgs0.append(wg)
+        load_front(1)
+        temp_t = keep.tile([P, PASSES, PACK], F32, name="temp_t")
+        nc.sync.dma_start(temp_t[:], temp.rearrange("(b p i) -> p b i", b=PASSES, i=PACK))
+        nc.sync.dma_start(idx3[:], offs3)
+        gain_t = keep.tile([P, PASSES, PACK], F32, name="gain_t")
+        nc.sync.dma_start(gain_t[:], gain.rearrange("(b p i) -> p b i", b=PASSES, i=PACK))
+        load_plan(0)
+        temp_c = temp_t[:].rearrange("p b i -> p (b i)")
+        gain_c = gain_t[:].rearrange("p b i -> p (b i)")
+        neg_temp = keep.tile([P, TILES], F32, name="neg_temp")
+        nc.scalar.activation(out=neg_temp[:], in_=temp_c, func=ACT.Copy, scale=-1.0)
+        top = keep.tile([P, TILES], F32, name="top")
+        bias = keep.tile([P, TILES], F32, name="bias")
+
+        w4w = keep.tile([P, PASSES, N], U32, name="w4w", align_bytes=64)
+        w4s = keep.tile([P, PASSES, N], U8, name="w4s", align_bytes=64)
+
+        def prepare_w4(b):
+            raw = keep.tile([P, PACK, N], F32, name="w4raw", tag="tabw%d" % b, align_bytes=64)
+            nc.sync.dma_start(raw[:], w4.rearrange("(b p i) n -> b p i n", b=PASSES, i=PACK)[b])
+            woven = ring2.tile([P, N, PACK], BF16, name="w4woven", align_bytes=64)
+            nc.scalar.copy(woven[:], raw[:].rearrange("p i n -> p n i"))
+            nc.vector.quantize_mx(
+                out=w4w[:, b, :].bitcast(FP8X4), scales=w4s[:, b, :], in_=woven[:].rearrange("p n i -> p (n i)")
+            )
+
+        f_woven = [keep.tile([P, PW, PACK], BF16, name="f_woven%d" % b, align_bytes=64) for b in range(PASSES)]
+        f_scales = keep.tile([P, PASSES, PW], U8, name="f_scales", align_bytes=64)
+
+        def bank(k):
+            return psum.tile([P, HALF], F32, name="bank%d" % k, tag="bank%d" % k)
+
+        def front(t):
+            h_t = ring2.tile([P, S], F32, name="h_t")
+            split = t % PACK == 0
+            for h in range(2):
+                acc = bank(2 * (t % PACK) + h)
+                for a in range(PASSES):
+                    nc.tensor.matmul_mx(
+                        out=acc[:],
+                        lhsT=w1w[:, a, 256 * t : 256 * (t + 1)].bitcast(FP4X4),
+                        lhsT_scale=w1s[:, a, P * t : P * (t + 1)],
+                        rhs=vw[a][h][:].bitcast(FP8X4),
+                        rhs_scale=vs[:, a, half(h)],
+                        start=(a == 0),
+                        stop=(a == PASSES - 1),
+                    )
+                st = stock0[h][:] if t == 0 else stock_t[t][:, half(h)]
+                nc.vector.tensor_tensor(h_t[:, half(h)], acc[:], st, ALU.add)
+                if split:
+                    nc.vector.tensor_tensor(
+                        page_t[t][:].indirect(idx2[:, list_half(h)]), h_t[:, half(h)], wgs0[h][:], ALU.mult
+                    )
+            if not split:
+                nc.vector.tensor_tensor(page_t[t][:].indirect(idx2[:]), h_t[:], wgs_t[t % PACK][:], ALU.mult)
+            nc.vector.reduce_max(top[:, t : t + 1], page_t[t][:], axis=AX.X)
+            nc.scalar.activation(
+                out=bias[:, t : t + 1], in_=top[:, t : t + 1], func=ACT.Copy, scale=neg_temp[:, t : t + 1]
+            )
+
+        def look(t, dst, offsets):
+            nc.scalar.activation(
+                out=dst, in_=page_t[t][:].indirect(offsets), func=ACT.Exp,
+                bias=bias[:, t : t + 1], scale=temp_c[:, t : t + 1],
+            )
+
+        def back(t):
+            a_t = ring2.tile([P, PW], F32, name="a_t")
+            look(t, a_t[:], idx3[:])
+            d_t = ring2.tile([P, PW], F32, name="d_t")
+            nc.gpsimd.tensor_tensor(d_t[:], a_t[:], plan_t[t][:], ALU.subtract)
+            nc.scalar.activation(
+                out=f_woven[t // PACK][:, :, t % PACK], in_=d_t[:], func=ACT.Copy, scale=gain_c[:, t : t + 1]
+            )
+
+        y = {}
+
+        def second(b, h, codes):
+            for n in range(N // P):
+                if b == 0:
+                    y[h, n] = bank(PACK * h + n)
+                nc.tensor.matmul_mx(
+                    out=y[h, n][:],
+                    lhsT=w4w[:, b, P * n : P * (n + 1)].bitcast(FP8X4),
+                    lhsT_scale=w4s[:, b, P * n : P * (n + 1)],
+                    rhs=codes.bitcast(FP8X4),
+                    rhs_scale=f_scales[:, b, half(h)],
+                    start=(b == 0),
+                    stop=(b == PASSES - 1),
+                )
+
+        floor_t = keep.tile([P, N // P], F32, name="floor_t")
+        for t in range(TILES - 2):
+            front(t)
+            back(t)
+            load_front(t + 2)
+            load_plan(t + 1)
+            if t in (1, 2):
+                prepare_w4(t - 1)
+            if t == 3:
+                with nc.allow_non_contiguous_dma(reason="one floor value to a partition"):
+                    nc.sync.dma_start(floor_t[:], floor.rearrange("(n p) -> p n", p=P))
+        load_plan(TILES - 1)
+
+        codes0 = keep.tile([P, PW], U32, name="codes0", tag="wgs1", align_bytes=64)
+        nc.vector.quantize_mx(
+            out=codes0[:].bitcast(FP8X4), scales=f_scales[:, 0, :], in_=f_woven[0][:].rearrange("p m i -> p (m i)")
+        )
+
+        t6, t7 = TILES - 2, TILES - 1
+        front(t6)
+        a6 = ring2.tile([P, PW], F32, name="a_t")
+        look(t6, a6[:], idx3[:])
+        front(t7)
+        for h in range(2):
+            second(0, h, codes0[:, half(h)])
+        d6 = keep.tile([P, PW], F32, name="d6", tag="wgs3", align_bytes=64)
+        nc.gpsimd.tensor_tensor(d6[:], a6[:], plan_t[t6][:], ALU.subtract)
+        a7 = [keep.tile([P, HALF], F32, name="a7_%d" % h) for h in range(2)]
+        for h in range(2):
+            look(t7, a7[h][:], idx3[:, list_half(h)])
+        nc.vector.tensor_scalar(f_woven[1][:, :, 2], d6[:], gain_c[:, t6 : t6 + 1], None, ALU.mult)
+        codes1 = keep.tile([P, PW], U32, name="codes1", align_bytes=64)
+        for h in range(2):
+            d7 = ring2.tile([P, HALF], F32, name="d7")
+            nc.vector.tensor_tensor(d7[:], a7[h][:], plan_t[t7][:, half(h)], ALU.subtract)
+            nc.vector.tensor_scalar(f_woven[1][:, half(h), 3], d7[:], gain_c[:, t7 : t7 + 1], None, ALU.mult)
+            nc.vector.quantize_mx(
+                out=codes1[:, half(h)].bitcast(FP8X4),
+                scales=f_scales[:, 1, half(h)],
+                in_=f_woven[1][:, half(h), :].rearrange("p m i -> p (m i)"),
+            )
+            second(1, h, codes1[:, half(h)])
+        for h in range(2):
+            for n in range(N // P):
+                res = keep.tile([P, HALF], F32, name="res%d%d" % (h, n))
+                if h == 0:
+                    sums = ring2.tile([P, HALF], F32, name="sums")
+                    nc.scalar.copy(sums[:], y[h, n][:])
+                    nc.gpsimd.tensor_scalar(res[:], sums[:], F32_MAX, floor_t[:, n : n + 1], ALU.min, ALU.max)
+                else:
+                    nc.vector.tensor_scalar(res[:], y[h, n][:], floor_t[:, n : n + 1], None, ALU.max)
+                nc.sync.dma_start(out[P * n : P * (n + 1), half(h)], res[:])

@@ -73,19 +73,19 @@ def tile_list_wave_bin_scores_kernel(
             tabw.append(tw)
 
         vs = keep.tile([P, PASSES, S], U8, name="vs", align_bytes=64)
-        nc.gpsimd.memset(vs[:], 0)
+        nc.vector.memset(vs[:].bitcast(I32), 0)
         gs = keep.tile([P, S], U8, name="gs", align_bytes=64)
         nc.vector.tensor_copy(gs[:], tabs[:].indirect(idx1[:]))
         for a in range(PASSES):
             for q in range(4):
                 src = 96 + 16 * a + 4 * q
-                nc.scalar.dma_start(vs[32 * q : 32 * q + 4, a, :].bitcast(I32), gs[src : src + 4, :].bitcast(I32))
+                nc.gpsimd.dma_start(vs[32 * q : 32 * q + 4, a, :].bitcast(I32), gs[src : src + 4, :].bitcast(I32))
 
         w1w = keep.tile([P, PASSES, 2 * H], U8, name="w1w", align_bytes=64)
         for a in range(PASSES):
-            nc.vector.tensor_copy(
-                w1w[:, a, :].rearrange("p (b i m e) -> p b i m e", b=PASSES, i=PACK, e=2),
-                w1w_raw[:, a, :].rearrange("p (b m i e) -> p b i m e", b=PASSES, i=PACK, e=2),
+            nc.scalar.copy(
+                w1w[:, a, :].bitcast(U16).rearrange("p (b i m) -> p b i m", b=PASSES, i=PACK),
+                w1w_raw[:, a, :].bitcast(U16).rearrange("p (b m i) -> p b i m", b=PASSES, i=PACK),
             )
         w1s = keep.tile([P, PASSES, H], U8, name="w1s", align_bytes=64)
         nc.vector.tensor_copy(
@@ -166,7 +166,10 @@ def tile_list_wave_bin_scores_kernel(
 
         def front(t):
             h_t = ring2.tile([P, S], F32, name="h_t")
-            split = t % PACK == 0
+            if t in (5, 7):
+                put = keep.tile([P, S], F32, name="put%d" % t, tag="put%d" % t, align_bytes=64)
+            else:
+                put = ring2.tile([P, S], F32, name="put")
             for h in range(2):
                 acc = bank(2 * (t % PACK) + h)
                 for a in range(PASSES):
@@ -179,14 +182,24 @@ def tile_list_wave_bin_scores_kernel(
                         start=(a == 0),
                         stop=(a == PASSES - 1),
                     )
-                st = stock0[h][:] if t == 0 else stock_t[t][:, half(h)]
-                nc.vector.tensor_tensor(h_t[:, half(h)], acc[:], st, ALU.add)
-                if split:
-                    nc.vector.tensor_tensor(
-                        page_t[t][:].indirect(idx2[:, list_half(h)]), h_t[:, half(h)], wgs0[h][:], ALU.mult
-                    )
-            if not split:
-                nc.vector.tensor_tensor(page_t[t][:].indirect(idx2[:]), h_t[:], wgs_t[t % PACK][:], ALU.mult)
+                if t > 0:
+                    nc.scalar.copy(h_t[:, half(h)], acc[:])
+                    continue
+                nc.vector.tensor_tensor(h_t[:, half(h)], acc[:], stock0[h][:], ALU.add)
+                window = page_t[t][:].indirect(idx2[:, list_half(h)])
+                if h == 0:
+                    nc.vector.tensor_tensor(window, h_t[:, half(h)], wgs0[h][:], ALU.mult)
+                else:
+                    nc.vector.tensor_tensor(put[:, half(h)], h_t[:, half(h)], wgs0[h][:], ALU.mult)
+                    nc.vector.tensor_copy(window, put[:, half(h)])
+            if t > 0:
+                nc.gpsimd.tensor_tensor(h_t[:], h_t[:], stock_t[t][:], ALU.add)
+                if t == PACK:
+                    for h in range(2):
+                        nc.gpsimd.tensor_tensor(put[:, half(h)], h_t[:, half(h)], wgs0[h][:], ALU.mult)
+                else:
+                    nc.gpsimd.tensor_tensor(put[:], h_t[:], wgs_t[t % PACK][:], ALU.mult)
+                nc.vector.tensor_copy(page_t[t][:].indirect(idx2[:]), put[:])
             nc.vector.reduce_max(top[:, t : t + 1], page_t[t][:], axis=AX.X)
             nc.scalar.activation(
                 out=bias[:, t : t + 1], in_=top[:, t : t + 1], func=ACT.Copy, scale=neg_temp[:, t : t + 1]
@@ -236,7 +249,7 @@ def tile_list_wave_bin_scores_kernel(
                     nc.sync.dma_start(floor_t[:], floor.rearrange("(n p) -> p n", p=P))
         load_plan(TILES - 1)
 
-        codes0 = keep.tile([P, PW], U32, name="codes0", tag="wgs1", align_bytes=64)
+        codes0 = keep.tile([P, PW], U32, name="codes0", tag="put5", align_bytes=64)
         nc.vector.quantize_mx(
             out=codes0[:].bitcast(FP8X4), scales=f_scales[:, 0, :], in_=f_woven[0][:].rearrange("p m i -> p (m i)")
         )
@@ -248,7 +261,7 @@ def tile_list_wave_bin_scores_kernel(
         front(t7)
         for h in range(2):
             second(0, h, codes0[:, half(h)])
-        d6 = keep.tile([P, PW], F32, name="d6", tag="wgs3", align_bytes=64)
+        d6 = keep.tile([P, PW], F32, name="d6", tag="put7", align_bytes=64)
         nc.gpsimd.tensor_tensor(d6[:], a6[:], plan_t[t6][:], ALU.subtract)
         a7 = [keep.tile([P, HALF], F32, name="a7_%d" % h) for h in range(2)]
         for h in range(2):
@@ -266,12 +279,13 @@ def tile_list_wave_bin_scores_kernel(
             )
             second(1, h, codes1[:, half(h)])
         for h in range(2):
+            res_h = keep.tile([P, N // P, HALF], F32, name="res%d" % h, tag="tabw%d" % h, align_bytes=64)
             for n in range(N // P):
-                res = keep.tile([P, HALF], F32, name="res%d%d" % (h, n))
+                res = res_h[:, n, :]
                 if h == 0:
                     sums = ring2.tile([P, HALF], F32, name="sums")
                     nc.scalar.copy(sums[:], y[h, n][:])
-                    nc.gpsimd.tensor_scalar(res[:], sums[:], F32_MAX, floor_t[:, n : n + 1], ALU.min, ALU.max)
+                    nc.gpsimd.tensor_scalar(res, sums[:], F32_MAX, floor_t[:, n : n + 1], ALU.min, ALU.max)
                 else:
-                    nc.vector.tensor_scalar(res[:], y[h, n][:], floor_t[:, n : n + 1], None, ALU.max)
-                nc.sync.dma_start(out[P * n : P * (n + 1), half(h)], res[:])
+                    nc.vector.tensor_scalar(res, y[h, n][:], floor_t[:, n : n + 1], None, ALU.max)
+                nc.sync.dma_start(out[P * n : P * (n + 1), half(h)], res)

@@ -146,17 +146,14 @@ def tile_list_wave_bin_scores_kernel(
         top = keep.tile([P, TILES], F32, name="top")
         bias = keep.tile([P, TILES], F32, name="bias")
 
-        w4w = keep.tile([P, PASSES, N], U32, name="w4w", align_bytes=64)
         w4s = keep.tile([P, PASSES, N], U8, name="w4s", align_bytes=64)
 
-        def prepare_w4(b):
+        def weave_w4(b):
             raw = keep.tile([P, PACK, N], F32, name="w4raw", tag="tabw%d" % b, align_bytes=64)
             nc.sync.dma_start(raw[:], w4.rearrange("(b p i) n -> b p i n", b=PASSES, i=PACK)[b])
             woven = ring2.tile([P, N, PACK], BF16, name="w4woven", align_bytes=64)
             nc.scalar.copy(woven[:], raw[:].rearrange("p i n -> p n i"))
-            nc.vector.quantize_mx(
-                out=w4w[:, b, :].bitcast(FP8X4), scales=w4s[:, b, :], in_=woven[:].rearrange("p n i -> p (n i)")
-            )
+            return woven
 
         f_woven = [keep.tile([P, PW, PACK], BF16, name="f_woven%d" % b, align_bytes=64) for b in range(PASSES)]
         f_scales = keep.tile([P, PASSES, PW], U8, name="f_scales", align_bytes=64)
@@ -164,42 +161,56 @@ def tile_list_wave_bin_scores_kernel(
         def bank(k):
             return psum.tile([P, HALF], F32, name="bank%d" % k, tag="bank%d" % k)
 
-        def front(t):
-            h_t = ring2.tile([P, S], F32, name="h_t")
-            if t in (5, 7):
-                put = keep.tile([P, S], F32, name="put%d" % t, tag="put%d" % t, align_bytes=64)
-            else:
-                put = ring2.tile([P, S], F32, name="put")
+        h_t, put_t, a_t = {}, {}, {}
+
+        def product(t, h):
+            acc = bank(2 * (t % PACK) + h)
+            for a in range(PASSES):
+                nc.tensor.matmul_mx(
+                    out=acc[:],
+                    lhsT=w1w[:, a, 256 * t : 256 * (t + 1)].bitcast(FP4X4),
+                    lhsT_scale=w1s[:, a, P * t : P * (t + 1)],
+                    rhs=vw[a][h][:].bitcast(FP8X4),
+                    rhs_scale=vs[:, a, half(h)],
+                    start=(a == 0),
+                    stop=(a == PASSES - 1),
+                )
+            return acc
+
+        def first_tile():
+            h0 = ring3.tile([P, S], F32, name="h_t")
+            put = ring2.tile([P, S], F32, name="put")
             for h in range(2):
-                acc = bank(2 * (t % PACK) + h)
-                for a in range(PASSES):
-                    nc.tensor.matmul_mx(
-                        out=acc[:],
-                        lhsT=w1w[:, a, 256 * t : 256 * (t + 1)].bitcast(FP4X4),
-                        lhsT_scale=w1s[:, a, P * t : P * (t + 1)],
-                        rhs=vw[a][h][:].bitcast(FP8X4),
-                        rhs_scale=vs[:, a, half(h)],
-                        start=(a == 0),
-                        stop=(a == PASSES - 1),
-                    )
-                if t > 0:
-                    nc.scalar.copy(h_t[:, half(h)], acc[:])
-                    continue
-                nc.vector.tensor_tensor(h_t[:, half(h)], acc[:], stock0[h][:], ALU.add)
-                window = page_t[t][:].indirect(idx2[:, list_half(h)])
+                acc = product(0, h)
+                nc.vector.tensor_tensor(h0[:, half(h)], acc[:], stock0[h][:], ALU.add)
+                window = page_t[0][:].indirect(idx2[:, list_half(h)])
                 if h == 0:
-                    nc.vector.tensor_tensor(window, h_t[:, half(h)], wgs0[h][:], ALU.mult)
+                    nc.vector.tensor_tensor(window, h0[:, half(h)], wgs0[h][:], ALU.mult)
                 else:
-                    nc.vector.tensor_tensor(put[:, half(h)], h_t[:, half(h)], wgs0[h][:], ALU.mult)
+                    nc.vector.tensor_tensor(put[:, half(h)], h0[:, half(h)], wgs0[h][:], ALU.mult)
                     nc.vector.tensor_copy(window, put[:, half(h)])
-            if t > 0:
-                nc.gpsimd.tensor_tensor(h_t[:], h_t[:], stock_t[t][:], ALU.add)
-                if t == PACK:
-                    for h in range(2):
-                        nc.gpsimd.tensor_tensor(put[:, half(h)], h_t[:, half(h)], wgs0[h][:], ALU.mult)
-                else:
-                    nc.gpsimd.tensor_tensor(put[:], h_t[:], wgs_t[t % PACK][:], ALU.mult)
-                nc.vector.tensor_copy(page_t[t][:].indirect(idx2[:]), put[:])
+
+        def empty_banks(t):
+            h_t[t] = ring3.tile([P, S], F32, name="h_t")
+            for h in range(2):
+                nc.scalar.copy(h_t[t][:, half(h)], product(t, h)[:])
+
+        def weigh(t):
+            if t in (5, 7):
+                put_t[t] = keep.tile([P, S], F32, name="put%d" % t, tag="put%d" % t, align_bytes=64)
+            else:
+                put_t[t] = ring2.tile([P, S], F32, name="put")
+            nc.gpsimd.tensor_tensor(h_t[t][:], h_t[t][:], stock_t[t][:], ALU.add)
+            if t == PACK:
+                for h in range(2):
+                    nc.gpsimd.tensor_tensor(put_t[t][:, half(h)], h_t[t][:, half(h)], wgs0[h][:], ALU.mult)
+            else:
+                nc.gpsimd.tensor_tensor(put_t[t][:], h_t[t][:], wgs_t[t % PACK][:], ALU.mult)
+
+        def scatter(t):
+            nc.vector.tensor_copy(page_t[t][:].indirect(idx2[:]), put_t[t][:])
+
+        def row_top(t):
             nc.vector.reduce_max(top[:, t : t + 1], page_t[t][:], axis=AX.X)
             nc.scalar.activation(
                 out=bias[:, t : t + 1], in_=top[:, t : t + 1], func=ACT.Copy, scale=neg_temp[:, t : t + 1]
@@ -211,18 +222,18 @@ def tile_list_wave_bin_scores_kernel(
                 bias=bias[:, t : t + 1], scale=temp_c[:, t : t + 1],
             )
 
-        def back(t):
-            a_t = ring2.tile([P, PW], F32, name="a_t")
-            look(t, a_t[:], idx3[:])
-            d_t = ring2.tile([P, PW], F32, name="d_t")
-            nc.gpsimd.tensor_tensor(d_t[:], a_t[:], plan_t[t][:], ALU.subtract)
+        def look_whole(t):
+            a_t[t] = ring2.tile([P, PW], F32, name="a_t")
+            look(t, a_t[t][:], idx3[:])
+
+        def weave(t):
             nc.scalar.activation(
-                out=f_woven[t // PACK][:, :, t % PACK], in_=d_t[:], func=ACT.Copy, scale=gain_c[:, t : t + 1]
+                out=f_woven[t // PACK][:, :, t % PACK], in_=h_t[t + 2][:], func=ACT.Copy, scale=gain_c[:, t : t + 1]
             )
 
         y = {}
 
-        def second(b, h, codes):
+        def second(b, h, w4w, codes):
             for n in range(N // P):
                 if b == 0:
                     y[h, n] = bank(PACK * h + n)
@@ -237,47 +248,74 @@ def tile_list_wave_bin_scores_kernel(
                 )
 
         floor_t = keep.tile([P, N // P], F32, name="floor_t")
+        t6, t7 = TILES - 2, TILES - 1
+        first_tile()
+        empty_banks(1)
+        weigh(1)
+        woven = {}
         for t in range(TILES - 2):
-            front(t)
-            back(t)
             load_front(t + 2)
+            empty_banks(t + 2)
+            if t > 0:
+                scatter(t)
+            weigh(t + 2)
+            row_top(t)
+            look_whole(t)
+            nc.gpsimd.tensor_tensor(h_t[t + 2][:], a_t[t][:], plan_t[t][:], ALU.subtract)
+            if t > 0:
+                weave(t - 1)
             load_plan(t + 1)
-            if t in (1, 2):
-                prepare_w4(t - 1)
+            if t in (1, 3):
+                woven[t // 2] = weave_w4(t // 2)
             if t == 3:
                 with nc.allow_non_contiguous_dma(reason="one floor value to a partition"):
                     nc.sync.dma_start(floor_t[:], floor.rearrange("(n p) -> p n", p=P))
         load_plan(TILES - 1)
 
-        codes0 = keep.tile([P, PW], U32, name="codes0", tag="put5", align_bytes=64)
-        nc.vector.quantize_mx(
-            out=codes0[:].bitcast(FP8X4), scales=f_scales[:, 0, :], in_=f_woven[0][:].rearrange("p m i -> p (m i)")
-        )
+        def quantize_f(b, h, codes):
+            nc.vector.quantize_mx(
+                out=codes.bitcast(FP8X4),
+                scales=f_scales[:, b, half(h)],
+                in_=f_woven[b][:, half(h), :].rearrange("p m i -> p (m i)"),
+            )
 
-        t6, t7 = TILES - 2, TILES - 1
-        front(t6)
-        a6 = ring2.tile([P, PW], F32, name="a_t")
-        look(t6, a6[:], idx3[:])
-        front(t7)
+        early = keep.tile([P, HALF], U32, name="early", tag="put5", align_bytes=64)
+        quantize_f(0, 0, early[:])
+
+        scatter(t6)
+        weave(t6 - 1)
+        row_top(t6)
+        a6 = [ring2.tile([P, HALF], F32, name="a6") for h in range(2)]
         for h in range(2):
-            second(0, h, codes0[:, half(h)])
-        d6 = keep.tile([P, PW], F32, name="d6", tag="put7", align_bytes=64)
-        nc.gpsimd.tensor_tensor(d6[:], a6[:], plan_t[t6][:], ALU.subtract)
+            look(t6, a6[h][:], idx3[:, list_half(h)])
+        for h in range(2):
+            d6 = ring2.tile([P, HALF], F32, name="d6")
+            nc.gpsimd.tensor_tensor(d6[:], a6[h][:], plan_t[t6][:, half(h)], ALU.subtract)
+            nc.scalar.activation(
+                out=f_woven[1][:, half(h), 2], in_=d6[:], func=ACT.Copy, scale=gain_c[:, t6 : t6 + 1]
+            )
+        scatter(t7)
+        row_top(t7)
         a7 = [keep.tile([P, HALF], F32, name="a7_%d" % h) for h in range(2)]
         for h in range(2):
             look(t7, a7[h][:], idx3[:, list_half(h)])
-        nc.vector.tensor_scalar(f_woven[1][:, :, 2], d6[:], gain_c[:, t6 : t6 + 1], None, ALU.mult)
+        late = keep.tile([P, PASSES + 1, N], U32, name="late", tag="put7", align_bytes=64)
+        w4w = late[:, 0:PASSES, :]
+        for b in range(PASSES):
+            nc.vector.quantize_mx(
+                out=w4w[:, b, :].bitcast(FP8X4), scales=w4s[:, b, :], in_=woven[b][:].rearrange("p n i -> p (n i)")
+            )
+            if b == 0:
+                second(0, 0, w4w, early[:])
+                quantize_f(0, 1, late[:, PASSES, :])
+                second(0, 1, w4w, late[:, PASSES, :])
         codes1 = keep.tile([P, PW], U32, name="codes1", align_bytes=64)
         for h in range(2):
-            d7 = ring2.tile([P, HALF], F32, name="d7")
+            d7 = keep.tile([P, HALF], F32, name="d7", tag="d7")
             nc.vector.tensor_tensor(d7[:], a7[h][:], plan_t[t7][:, half(h)], ALU.subtract)
             nc.vector.tensor_scalar(f_woven[1][:, half(h), 3], d7[:], gain_c[:, t7 : t7 + 1], None, ALU.mult)
-            nc.vector.quantize_mx(
-                out=codes1[:, half(h)].bitcast(FP8X4),
-                scales=f_scales[:, 1, half(h)],
-                in_=f_woven[1][:, half(h), :].rearrange("p m i -> p (m i)"),
-            )
-            second(1, h, codes1[:, half(h)])
+            quantize_f(1, h, codes1[:, half(h)])
+            second(1, h, w4w, codes1[:, half(h)])
         for h in range(2):
             res_h = keep.tile([P, N // P, HALF], F32, name="res%d" % h, tag="tabw%d" % h, align_bytes=64)
             for n in range(N // P):

@@ -15,7 +15,6 @@ FP8X4 = mybir.dt.float8_e4m3fn_x4
 FP4X4 = mybir.dt.float4_e2m1fn_x4
 ALU = mybir.AluOpType
 ACT = mybir.ActivationFunctionType
-AX = mybir.AxisListType
 
 P = 128
 PACK = 4
@@ -64,8 +63,18 @@ def tile_list_wave_bin_scores_kernel(
                 w1s_raw[32 * q : 32 * q + 4, :, :].bitcast(I32),
                 w1_scales[:, 4 * q : 4 * q + 4, :].rearrange("a r c -> r a c").bitcast(I32),
             )
-        w1w_raw = keep.tile([P, PASSES, 2 * H], U8, name="w1w_raw", align_bytes=64)
-        nc.sync.dma_start(w1w_raw[:].bitcast(I32), w1_words.rearrange("a p n -> p a n").bitcast(I32))
+        w1w = {}
+
+        def load_w1(b):
+            raw = keep.tile([P, PASSES, H], U8, name="w1w_raw%d" % b, align_bytes=64)
+            nc.sync.dma_start(raw[:].bitcast(I32), w1_words.rearrange("a p (b n) -> b p a n", b=PASSES)[b].bitcast(I32))
+            w1w[b] = keep.tile([P, PASSES, H], U8, name="w1w%d" % b, align_bytes=64)
+            nc.scalar.copy(
+                w1w[b][:].bitcast(U16).rearrange("p a (i m) -> p a i m", i=PACK),
+                raw[:].bitcast(U16).rearrange("p a (m i) -> p a i m", i=PACK),
+            )
+
+        load_w1(0)
         tabw = []
         for a in range(PASSES):
             tw = keep.tile([P, T], U32, name="tabw%d" % a, tag="tabw%d" % a, align_bytes=64)
@@ -81,12 +90,6 @@ def tile_list_wave_bin_scores_kernel(
                 src = 96 + 16 * a + 4 * q
                 nc.gpsimd.dma_start(vs[32 * q : 32 * q + 4, a, :].bitcast(I32), gs[src : src + 4, :].bitcast(I32))
 
-        w1w = keep.tile([P, PASSES, 2 * H], U8, name="w1w", align_bytes=64)
-        for a in range(PASSES):
-            nc.scalar.copy(
-                w1w[:, a, :].bitcast(U16).rearrange("p (b i m) -> p b i m", b=PASSES, i=PACK),
-                w1w_raw[:, a, :].bitcast(U16).rearrange("p (b m i) -> p b i m", b=PASSES, i=PACK),
-            )
         w1s = keep.tile([P, PASSES, H], U8, name="w1s", align_bytes=64)
         nc.vector.tensor_copy(
             w1s[:].rearrange("p a (b i m) -> p (a b) i m", b=PASSES, i=PACK),
@@ -107,7 +110,7 @@ def tile_list_wave_bin_scores_kernel(
             nc.sync.dma_start(stock_t[t][:], rows(stock, t))
             if t < PACK:
                 wgs_t[t] = keep.tile([P, S], F32, name="wgs%d" % t, tag="wgs%d" % t, align_bytes=64)
-                for q in range(4):
+                for q in (0, 2, 1, 3):
                     nc.sync.dma_start(
                         wgs_t[t][32 * q : 32 * q + 32, :], wgs.rearrange("(u i) c -> i u c", i=PACK)[t]
                     )
@@ -123,7 +126,7 @@ def tile_list_wave_bin_scores_kernel(
             st = keep.tile([P, HALF], F32, name="stock0_%d" % h)
             nc.sync.dma_start(st[:], rows(stock, 0)[:, half(h)])
             wg = keep.tile([P, HALF], F32, name="wgs0_%d" % h)
-            for q in range(4):
+            for q in (0, 2, 1, 3):
                 nc.sync.dma_start(
                     wg[32 * q : 32 * q + 32, :], wgs.rearrange("(u i) c -> i u c", i=PACK)[0][:, half(h)]
                 )
@@ -133,6 +136,7 @@ def tile_list_wave_bin_scores_kernel(
             stock0.append(st)
             wgs0.append(wg)
         load_front(1)
+        load_w1(1)
         temp_t = keep.tile([P, PASSES, PACK], F32, name="temp_t")
         nc.sync.dma_start(temp_t[:], temp.rearrange("(b p i) -> p b i", b=PASSES, i=PACK))
         nc.sync.dma_start(idx3[:], offs3)
@@ -143,7 +147,7 @@ def tile_list_wave_bin_scores_kernel(
         gain_c = gain_t[:].rearrange("p b i -> p (b i)")
         neg_temp = keep.tile([P, TILES], F32, name="neg_temp")
         nc.scalar.activation(out=neg_temp[:], in_=temp_c, func=ACT.Copy, scale=-1.0)
-        top = keep.tile([P, TILES], F32, name="top")
+        scaled = keep.tile([P, T2], BF16, name="scaled")
         bias = keep.tile([P, TILES], F32, name="bias")
 
         w4s = keep.tile([P, PASSES, N], U8, name="w4s", align_bytes=64)
@@ -155,7 +159,7 @@ def tile_list_wave_bin_scores_kernel(
             nc.scalar.copy(woven[:], raw[:].rearrange("p i n -> p n i"))
             return woven
 
-        f_woven = [keep.tile([P, PW, PACK], BF16, name="f_woven%d" % b, align_bytes=64) for b in range(PASSES)]
+        f_woven = [keep.tile([P, PW, PACK], BF16, name="f_woven%d" % b, tag="f_woven%d" % b, align_bytes=64) for b in range(PASSES)]
         f_scales = keep.tile([P, PASSES, PW], U8, name="f_scales", align_bytes=64)
 
         def bank(k):
@@ -168,7 +172,7 @@ def tile_list_wave_bin_scores_kernel(
             for a in range(PASSES):
                 nc.tensor.matmul_mx(
                     out=acc[:],
-                    lhsT=w1w[:, a, 256 * t : 256 * (t + 1)].bitcast(FP4X4),
+                    lhsT=w1w[t // PACK][:, a, 256 * (t % PACK) : 256 * (t % PACK + 1)].bitcast(FP4X4),
                     lhsT_scale=w1s[:, a, P * t : P * (t + 1)],
                     rhs=vw[a][h][:].bitcast(FP8X4),
                     rhs_scale=vs[:, a, half(h)],
@@ -211,9 +215,8 @@ def tile_list_wave_bin_scores_kernel(
             nc.vector.tensor_copy(page_t[t][:].indirect(idx2[:]), put_t[t][:])
 
         def row_top(t):
-            nc.vector.reduce_max(top[:, t : t + 1], page_t[t][:], axis=AX.X)
-            nc.scalar.activation(
-                out=bias[:, t : t + 1], in_=top[:, t : t + 1], func=ACT.Copy, scale=neg_temp[:, t : t + 1]
+            nc.vector.tensor_scalar(
+                scaled[:], page_t[t][:], neg_temp[:, t : t + 1], None, ALU.mult, ALU.min, accum_out=bias[:, t : t + 1]
             )
 
         def look(t, dst, offsets):
@@ -316,14 +319,16 @@ def tile_list_wave_bin_scores_kernel(
             nc.vector.tensor_scalar(f_woven[1][:, half(h), 3], d7[:], gain_c[:, t7 : t7 + 1], None, ALU.mult)
             quantize_f(1, h, codes1[:, half(h)])
             second(1, h, w4w, codes1[:, half(h)])
+        res = [
+            keep.tile([P, N // P, HALF], F32, name="res%d" % h, tag="f_woven%d" % (1 - h), align_bytes=64)
+            for h in range(2)
+        ]
         for h in range(2):
-            res_h = keep.tile([P, N // P, HALF], F32, name="res%d" % h, tag="tabw%d" % h, align_bytes=64)
             for n in range(N // P):
-                res = res_h[:, n, :]
-                if h == 0:
-                    sums = ring2.tile([P, HALF], F32, name="sums")
+                if h == 0 and n < 3:
+                    sums = ring3.tile([P, HALF], F32, name="sums")
                     nc.scalar.copy(sums[:], y[h, n][:])
-                    nc.gpsimd.tensor_scalar(res, sums[:], F32_MAX, floor_t[:, n : n + 1], ALU.min, ALU.max)
+                    nc.gpsimd.tensor_scalar(res[h][:, n, :], sums[:], F32_MAX, floor_t[:, n : n + 1], ALU.min, ALU.max)
                 else:
-                    nc.vector.tensor_scalar(res, y[h, n][:], floor_t[:, n : n + 1], None, ALU.max)
-                nc.sync.dma_start(out[P * n : P * (n + 1), half(h)], res)
+                    nc.vector.tensor_scalar(res[h][:, n, :], y[h, n][:], floor_t[:, n : n + 1], None, ALU.max)
+                nc.sync.dma_start(out[P * n : P * (n + 1), half(h)], res[h][:, n, :])

from contextlib import ExitStack

import concourse.mybir as mybir

K, H, N, T, S, T2, PW = 1024, 1024, 512, 4096, 1024, 2048, 1024
FLOPS = 2 * K * H * S + 2 * H * N * PW

F32 = mybir.dt.float32
BF16 = mybir.dt.bfloat16
I32 = mybir.dt.int32
U32 = mybir.dt.uint32
U16 = mybir.dt.uint16
U8 = mybir.dt.uint8
FP8X4 = mybir.dt.float8_e4m3fn_x4
FP4X4 = mybir.dt.float4_e2m1fn_x4
ALU = mybir.AluOpType
ACT = mybir.ActivationFunctionType

P = 128
PACK = 4
PASSES = 2
TILES = PASSES * PACK
HALF = 512
LIST_HALF = HALF // 16
F32_MAX = 3.4028234663852886e38


def tile_list_wave_bin_scores_kernel(
    tc, tab_words, tab_scales, offs, offs2, offs3, w1_words, w1_scales,
    stock, page0, wgs, temp, plan, gain, w4, floor, out,
):
    nc = tc.nc
    with ExitStack() as ctx:
        lists = ctx.enter_context(tc.tile_pool(name="lists", bufs=1))
        keep = ctx.enter_context(tc.tile_pool(name="keep", bufs=1))
        ring2 = ctx.enter_context(tc.tile_pool(name="ring2", bufs=2))
        ring3 = ctx.enter_context(tc.tile_pool(name="ring3", bufs=3))
        ring4 = ctx.enter_context(tc.tile_pool(name="ring4", bufs=4))
        psum = ctx.enter_context(tc.psum_pool(name="psum", bufs=1))

        def rows(mat, t):
            return mat.rearrange("(b p i) c -> b i p c", b=PASSES, i=PACK)[t // PACK, t % PACK]

        def half(h):
            return slice(h * HALF, (h + 1) * HALF)

        def list_half(h):
            return slice(h * LIST_HALF, (h + 1) * LIST_HALF)

        idx1 = lists.tile([P, S // 16], U16, name="idx1")
        idx2 = lists.tile([P, S // 16], U16, name="idx2")
        idx3 = lists.tile([P, PW // 16], U16, name="idx3")
        nc.sync.dma_start(idx1[:], offs)
        nc.sync.dma_start(idx2[:], offs2)

        w1s_raw = keep.tile([P, PASSES, H], U8, name="w1s_raw", align_bytes=64)
        nc.vector.memset(w1s_raw[:].bitcast(I32), 0)
        tabs = keep.tile([P, T], U8, name="tabs", align_bytes=64)
        nc.vector.memset(tabs[0:96, :].bitcast(I32), 0)
        nc.sync.dma_start(tabs[96:128, :].bitcast(I32), tab_scales.rearrange("a q t -> (a q) t").bitcast(I32))
        for q in range(4):
            nc.scalar.dma_start(
                w1s_raw[32 * q : 32 * q + 4, :, :].bitcast(I32),
                w1_scales[:, 4 * q : 4 * q + 4, :].rearrange("a r c -> r a c").bitcast(I32),
            )
        w1w = {}

        def load_w1(b):
            raw = keep.tile([P, PASSES, H], U8, name="w1w_raw%d" % b, align_bytes=64)
            nc.sync.dma_start(raw[:].bitcast(I32), w1_words.rearrange("a p (b n) -> b p a n", b=PASSES)[b].bitcast(I32))
            w1w[b] = keep.tile([P, PASSES, H], U8, name="w1w%d" % b, align_bytes=64)
            nc.scalar.copy(
                w1w[b][:].bitcast(U16).rearrange("p a (i m) -> p a i m", i=PACK),
                raw[:].bitcast(U16).rearrange("p a (m i) -> p a i m", i=PACK),
            )

        load_w1(0)
        tabw = []
        for a in range(PASSES):
            tw = keep.tile([P, T], U32, name="tabw%d" % a, tag="tabw%d" % a, align_bytes=64)
            nc.sync.dma_start(tw[:].bitcast(I32), tab_words[a].rearrange("p t i -> p (t i)").bitcast(I32))
            tabw.append(tw)

        vs = keep.tile([P, PASSES, S], U8, name="vs", align_bytes=64)
        nc.vector.memset(vs[:].bitcast(I32), 0)
        gs = keep.tile([P, S], U8, name="gs", align_bytes=64)
        nc.vector.tensor_copy(gs[:], tabs[:].indirect(idx1[:]))
        for a in range(PASSES):
            for q in range(4):
                src = 96 + 16 * a + 4 * q
                nc.gpsimd.dma_start(vs[32 * q : 32 * q + 4, a, :].bitcast(I32), gs[src : src + 4, :].bitcast(I32))

        w1s = keep.tile([P, PASSES, H], U8, name="w1s", align_bytes=64)
        nc.vector.tensor_copy(
            w1s[:].rearrange("p a (b i m) -> p (a b) i m", b=PASSES, i=PACK),
            w1s_raw[:].rearrange("p a (b m i) -> p (a b) i m", b=PASSES, i=PACK),
        )

        vw = [[None, None], [None, None]]
        for a in range(PASSES):
            for h in range(2):
                g = keep.tile([P, HALF], U32, name="vw%d%d" % (a, h), align_bytes=64)
                nc.vector.tensor_copy(g[:], tabw[a][:].indirect(idx1[:, list_half(h)]))
                vw[a][h] = g

        stock_t, wgs_t, page_t, plan_t = {}, {}, {}, {}

        def load_front(t):
            stock_t[t] = ring3.tile([P, S], F32, name="stock")
            nc.sync.dma_start(stock_t[t][:], rows(stock, t))
            if t < PACK:
                wgs_t[t] = keep.tile([P, S], F32, name="wgs%d" % t, tag="wgs%d" % t, align_bytes=64)
                for q in (0, 2, 1, 3):
                    nc.sync.dma_start(
                        wgs_t[t][32 * q : 32 * q + 32, :], wgs.rearrange("(u i) c -> i u c", i=PACK)[t]
                    )
            page_t[t] = ring4.tile([P, T2], F32, name="page")
            nc.sync.dma_start(page_t[t][:], rows(page0, t))

        def load_plan(t):
            plan_t[t] = ring3.tile([P, PW], F32, name="plan")
            nc.sync.dma_start(plan_t[t][:], rows(plan, t))

        stock0, wgs0 = [], []
        for h in range(2):
            st = keep.tile([P, HALF], F32, name="stock0_%d" % h)
            nc.sync.dma_start(st[:], rows(stock, 0)[:, half(h)])
            wg = keep.tile([P, HALF], F32, name="wgs0_%d" % h)
            for q in (0, 2, 1, 3):
                nc.sync.dma_start(
                    wg[32 * q : 32 * q + 32, :], wgs.rearrange("(u i) c -> i u c", i=PACK)[0][:, half(h)]
                )
            if h == 0:
                page_t[0] = ring4.tile([P, T2], F32, name="page")
                nc.sync.dma_start(page_t[0][:], rows(page0, 0))
            stock0.append(st)
            wgs0.append(wg)
        load_front(1)
        load_w1(1)
        temp_t = keep.tile([P, PASSES, PACK], F32, name="temp_t")
        nc.sync.dma_start(temp_t[:], temp.rearrange("(b p i) -> p b i", b=PASSES, i=PACK))
        nc.sync.dma_start(idx3[:], offs3)
        gain_t = keep.tile([P, PASSES, PACK], F32, name="gain_t")
        nc.sync.dma_start(gain_t[:], gain.rearrange("(b p i) -> p b i", b=PASSES, i=PACK))
        load_plan(0)
        temp_c = temp_t[:].rearrange("p b i -> p (b i)")
        gain_c = gain_t[:].rearrange("p b i -> p (b i)")
        neg_temp = keep.tile([P, TILES], F32, name="neg_temp")
        nc.scalar.activation(out=neg_temp[:], in_=temp_c, func=ACT.Copy, scale=-1.0)
        scaled = keep.tile([P, T2], BF16, name="scaled")
        bias = keep.tile([P, TILES], F32, name="bias")

        w4s = keep.tile([P, PASSES, N], U8, name="w4s", align_bytes=64)

        def weave_w4(b):
            raw = keep.tile([P, PACK, N], F32, name="w4raw", tag="tabw%d" % b, align_bytes=64)
            nc.sync.dma_start(raw[:], w4.rearrange("(b p i) n -> b p i n", b=PASSES, i=PACK)[b])
            woven = ring2.tile([P, N, PACK], BF16, name="w4woven", align_bytes=64)
            nc.scalar.copy(woven[:], raw[:].rearrange("p i n -> p n i"))
            return woven

        f_woven = [keep.tile([P, PW, PACK], BF16, name="f_woven%d" % b, tag="f_woven%d" % b, align_bytes=64) for b in range(PASSES)]
        f_scales = keep.tile([P, PASSES, PW], U8, name="f_scales", align_bytes=64)

        def bank(k):
            return psum.tile([P, HALF], F32, name="bank%d" % k, tag="bank%d" % k)

        h_t, put_t, a_t = {}, {}, {}

        def product(t, h):
            acc = bank(2 * (t % PACK) + h)
            for a in range(PASSES):
                nc.tensor.matmul_mx(
                    out=acc[:],
                    lhsT=w1w[t // PACK][:, a, 256 * (t % PACK) : 256 * (t % PACK + 1)].bitcast(FP4X4),
                    lhsT_scale=w1s[:, a, P * t : P * (t + 1)],
                    rhs=vw[a][h][:].bitcast(FP8X4),
                    rhs_scale=vs[:, a, half(h)],
                    start=(a == 0),
                    stop=(a == PASSES - 1),
                )
            return acc

        def first_tile():
            h0 = ring3.tile([P, S], F32, name="h_t")
            put = ring2.tile([P, S], F32, name="put")
            for h in range(2):
                acc = product(0, h)
                nc.vector.tensor_tensor(h0[:, half(h)], acc[:], stock0[h][:], ALU.add)
                window = page_t[0][:].indirect(idx2[:, list_half(h)])
                if h == 0:
                    nc.vector.tensor_tensor(window, h0[:, half(h)], wgs0[h][:], ALU.mult)
                else:
                    nc.vector.tensor_tensor(put[:, half(h)], h0[:, half(h)], wgs0[h][:], ALU.mult)
                    nc.vector.tensor_copy(window, put[:, half(h)])

        def empty_banks(t):
            h_t[t] = ring3.tile([P, S], F32, name="h_t")
            for h in range(2):
                nc.scalar.copy(h_t[t][:, half(h)], product(t, h)[:])

        def weigh(t):
            if t in (5, 7):
                put_t[t] = keep.tile([P, S], F32, name="put%d" % t, tag="put%d" % t, align_bytes=64)
            else:
                put_t[t] = ring2.tile([P, S], F32, name="put")
            nc.gpsimd.tensor_tensor(h_t[t][:], h_t[t][:], stock_t[t][:], ALU.add)
            if t == PACK:
                for h in range(2):
                    nc.gpsimd.tensor_tensor(put_t[t][:, half(h)], h_t[t][:, half(h)], wgs0[h][:], ALU.mult)
            else:
                nc.gpsimd.tensor_tensor(put_t[t][:], h_t[t][:], wgs_t[t % PACK][:], ALU.mult)

        def scatter(t):
            nc.vector.tensor_copy(page_t[t][:].indirect(idx2[:]), put_t[t][:])

        def row_top(t):
            nc.vector.tensor_scalar(
                scaled[:], page_t[t][:], neg_temp[:, t : t + 1], None, ALU.mult, ALU.min, accum_out=bias[:, t : t + 1]
            )

        def look(t, dst, offsets):
            nc.scalar.activation(
                out=dst, in_=page_t[t][:].indirect(offsets), func=ACT.Exp,
                bias=bias[:, t : t + 1], scale=temp_c[:, t : t + 1],
            )

        def look_whole(t):
            a_t[t] = ring2.tile([P, PW], F32, name="a_t")
            look(t, a_t[t][:], idx3[:])

        def weave(t):
            nc.scalar.activation(
                out=f_woven[t // PACK][:, :, t % PACK], in_=h_t[t + 2][:], func=ACT.Copy, scale=gain_c[:, t : t + 1]
            )

        y = {}

        def second(b, h, w4w, codes):
            for n in range(N // P):
                if b == 0:
                    y[h, n] = bank(PACK * h + n)
                nc.tensor.matmul_mx(
                    out=y[h, n][:],
                    lhsT=w4w[:, b, P * n : P * (n + 1)].bitcast(FP8X4),
                    lhsT_scale=w4s[:, b, P * n : P * (n + 1)],
                    rhs=codes.bitcast(FP8X4),
                    rhs_scale=f_scales[:, b, half(h)],
                    start=(b == 0),
                    stop=(b == PASSES - 1),
                )

        floor_t = keep.tile([P, N // P], F32, name="floor_t")
        t6, t7 = TILES - 2, TILES - 1
        first_tile()
        empty_banks(1)
        weigh(1)
        woven = {}
        for t in range(TILES - 2):
            load_front(t + 2)
            empty_banks(t + 2)
            if t > 0:
                scatter(t)
            weigh(t + 2)
            row_top(t)
            look_whole(t)
            nc.gpsimd.tensor_tensor(h_t[t + 2][:], a_t[t][:], plan_t[t][:], ALU.subtract)
            if t > 0:
                weave(t - 1)
            load_plan(t + 1)
            if t in (1, 3):
                woven[t // 2] = weave_w4(t // 2)
            if t == 3:
                with nc.allow_non_contiguous_dma(reason="one floor value to a partition"):
                    nc.sync.dma_start(floor_t[:], floor.rearrange("(n p) -> p n", p=P))
        load_plan(TILES - 1)

        def quantize_f(b, h, codes):
            nc.vector.quantize_mx(
                out=codes.bitcast(FP8X4),
                scales=f_scales[:, b, half(h)],
                in_=f_woven[b][:, half(h), :].rearrange("p m i -> p (m i)"),
            )

        early = keep.tile([P, HALF], U32, name="early", tag="put5", align_bytes=64)
        quantize_f(0, 0, early[:])

        scatter(t6)
        weave(t6 - 1)
        row_top(t6)
        a6 = [ring2.tile([P, HALF], F32, name="a6") for h in range(2)]
        for h in range(2):
            look(t6, a6[h][:], idx3[:, list_half(h)])
        for h in range(2):
            d6 = ring2.tile([P, HALF], F32, name="d6")
            nc.gpsimd.tensor_tensor(d6[:], a6[h][:], plan_t[t6][:, half(h)], ALU.subtract)
            nc.scalar.activation(
                out=f_woven[1][:, half(h), 2], in_=d6[:], func=ACT.Copy, scale=gain_c[:, t6 : t6 + 1]
            )
        scatter(t7)
        row_top(t7)
        a7 = [keep.tile([P, HALF], F32, name="a7_%d" % h) for h in range(2)]
        for h in range(2):
            look(t7, a7[h][:], idx3[:, list_half(h)])
        late = keep.tile([P, PASSES + 1, N], U32, name="late", tag="put7", align_bytes=64)
        w4w = late[:, 0:PASSES, :]
        for b in range(PASSES):
            nc.vector.quantize_mx(
                out=w4w[:, b, :].bitcast(FP8X4), scales=w4s[:, b, :], in_=woven[b][:].rearrange("p n i -> p (n i)")
            )
            if b == 0:
                second(0, 0, w4w, early[:])
                quantize_f(0, 1, late[:, PASSES, :])
                second(0, 1, w4w, late[:, PASSES, :])
        codes1 = keep.tile([P, PW], U32, name="codes1", align_bytes=64)
        for h in range(2):
            d7 = keep.tile([P, HALF], F32, name="d7", tag="d7")
            nc.vector.tensor_tensor(d7[:], a7[h][:], plan_t[t7][:, half(h)], ALU.subtract)
            nc.vector.tensor_scalar(f_woven[1][:, half(h), 3], d7[:], gain_c[:, t7 : t7 + 1], None, ALU.mult)
            quantize_f(1, h, codes1[:, half(h)])
            second(1, h, w4w, codes1[:, half(h)])
        res = [
            keep.tile([P, N // P, HALF], F32, name="res%d" % h, tag="f_woven%d" % (1 - h), align_bytes=64)
            for h in range(2)
        ]
        for h in range(2):
            for n in range(N // P):
                if h == 0 and n < 3:
                    sums = ring3.tile([P, HALF], F32, name="sums")
                    nc.scalar.copy(sums[:], y[h, n][:])
                    nc.gpsimd.tensor_scalar(res[h][:, n, :], sums[:], F32_MAX, floor_t[:, n : n + 1], ALU.min, ALU.max)
                else:
                    nc.vector.tensor_scalar(res[h][:, n, :], y[h, n][:], floor_t[:, n : n + 1], None, ALU.max)
                nc.sync.dma_start(out[P * n : P * (n + 1), half(h)], res[h][:, n, :])
